import numpy as np, ml_dtypes
CORES = [56,61,80,85]
N = 4
import mx_ref
NC = 512
LR = np.float32(0.0645)
BF = ml_dtypes.bfloat16
def cut(t, i, w=512):
    return t[:, w * i:w * i + w]
def tile(rs):
    return np.stack(rs, axis=2).reshape(128, -1).astype(BF)
def pick(b):
    s = np.zeros((128, 128, 4), np.float32)
    s[np.arange(128), np.arange(128), b] = 1.0
    return mx_ref.quantize(s.reshape(128, 512).astype(BF))
def setup_inputs(rng):
    def f(*shape):
        return mx_ref.flush((rng.standard_normal(shape, dtype=np.float32) * np.exp2(rng.integers(-2, 3, shape[:-1] + (1,)))).astype(BF))
    return {"b": f(N, 128, N * 512), "w": f(N, 128, 512), "x": f(N, 128, 4 * NC)}
def setup_inputs_blocks(rng):
    d = setup_inputs(rng)
    for k in ("b", "w", "x"): d[k] = mx_ref.spread(d[k], rng, 2)
    return d
def setup_inputs_wide(rng):
    d = setup_inputs(rng)
    for k in ("b", "w", "x"): d[k] = mx_ref.flush((d[k].astype(np.float32) * np.exp2(rng.integers(-4, 5, (N, 1, 1))).astype(np.float32)).astype(BF))
    return d
def reference(b, w, x, own=None):
    S = [pick(t) for t in range(4)]
    h = np.zeros((N, 128, 512), BF)
    for c in range(N):
        for r in range(N):
            q = mx_ref.quantize(cut(b[r], c))
            P = [mx_ref.matmul(S[t], q) for t in range(4)]
            Z = P if r == 0 else [z + p for z, p in zip(Z, P)]
        h[c] = tile([w[c].astype(np.float32)[:, t::4] - Z[t] * LR for t in range(4)])
    use = h if own is None else own["h"]
    H = [mx_ref.quantize(use[j]) for j in range(N)]
    y = np.zeros((N, 128, N * NC), np.float32)
    for r in range(N):
        qx = mx_ref.quantize(x[r])
        for j in range(N):
            y[r][:, NC * j:NC * j + NC] = mx_ref.matmul(H[j], qx)
    return {"h": h, "y": y}

@@ -1,0 +1,195 @@
+from concourse.bass import DstId, RemoteDMATransfer
+from concourse.mybir import dt, AluOpType, ActivationFunctionType
+
+F8 = "float8_e4m3fn_x4"
+SCRATCH = {
+    "bt": ("sbuf", [128, 2048], "bfloat16"),
+    "wt": ("sbuf", [128, 512], "bfloat16"),
+    "xt": ("sbuf", [128, 2048], "bfloat16"),
+    "ones": ("sbuf", [128, 516], "bfloat16"),
+    "sel": ("sbuf", [128, 516], "bfloat16"),
+    "ht": ("sbuf", [128, 512], "bfloat16"),
+    "tm": ("sbuf", [128, 512], "float32"),
+    "yt": ("sbuf", [128, 2048], "float32"),
+    "cb": ("sbuf", [128, 512], F8), "sb": ("sbuf", [128, 512], "uint8"),
+    "cs": ("sbuf", [128, 512], F8), "ss": ("sbuf", [128, 512], "uint8"),
+    "cx": ("sbuf", [128, 512], F8), "sx": ("sbuf", [128, 512], "uint8"),
+    "cg": ("sbuf", [128, 512], F8), "sg": ("sbuf", [128, 512], "uint8"),
+    "ch": ("sbuf", [128, 512], F8), "sh": ("sbuf", [128, 512], "uint8"),
+    "acc": ("psum", [128, 4096], "float32"),
+    "rcg": ("sbuf", [128, 128], F8), "rsg": ("sbuf", [128, 128], "uint8"),
+    "rch": ("sbuf", [128, 128], F8), "rsh": ("sbuf", [128, 128], "uint8"),
+}
+SEMAPHORES = (["ldf", "ldn", "ldw", "ldx", "one", "sel", "qf", "qn", "qs", "qx", "rr", "qh", "sth", "left"]
+              + ["rgs", "rgc", "rhc", "rhs"]
+              + ["ga%d" % r for r in range(4)] + ["ha%d" % r for r in range(4)]
+              + ["z%d" % b for b in range(4)] + ["m%d" % b for b in range(4)]
+              + ["p%d%d" % (j, k) for j in range(4) for k in range(2)]
+              + ["d%d%d" % (j, k) for j in range(4) for k in range(2)] + ["sty0", "sty1"])
+LR = 0.0645
+
+
+def bits(m):
+    return [i for i in range(m.bit_length()) if (m >> i) & 1]
+
+
+def mask_of(es):
+    return sum(1 << e for e in es)
+
+
+def t_send(topo, dst, es, src_ap, dst_ap, sem):
+    rid, pid, _ = topo.addr(dst)
+    return RemoteDMATransfer(dst_ids=[DstId(rid=rid, pnc=pid)], dma_engine_mask=mask_of(es), remote_sem=sem,
+                             src=src_ap, dst=dst_ap)
+
+
+def plan(cores, r, topo):
+    me = cores[r]
+    near = [q for q in range(len(cores)) if q != r and topo.chip(cores[q]) == topo.chip(me)]
+    far = [q for q in range(len(cores)) if topo.chip(cores[q]) != topo.chip(me)]
+    hosts = [c for c in range(96) if topo.chip(c) == topo.chip(me) and topo.die(c) == topo.die(me) and c not in cores
+             and all(topo.may_write(c, cores[q]) for q in far)]
+    return near[0], far, hosts[:len(far)]
+
+
+def c8(t, a):
+    return t[:, a:a + 128].bitcast(dt.uint8)
+
+
+def relay_program(g, core, T, topo, r, dst):
+    S = T.sem
+    es = bits(topo.mask(core, T.cores[dst]))
+    rid, pid, _ = topo.addr(T.cores[dst])
+    m, n = mask_of(es), len(es)
+    g.wait_ge(S.rgs, 4)
+    g.remote_dma(T.sg[:, 128 * r:128 * r + 128], T.rsg[:, 0:128], S["ga%d" % r], S.left, pid, rid, m)
+    g.wait_ge(S.rgc, 4)
+    g.remote_dma(c8(T.cg, 128 * r), c8(T.rcg, 0), S["ga%d" % r], S.left, pid, rid, m)
+    g.wait_ge(S.rhc, 8)
+    g.remote_dma(c8(T.ch, 128 * r), c8(T.rch, 0), S["ha%d" % r], S.left, pid, rid, m)
+    g.wait_ge(S.rhs, 8)
+    g.remote_dma(T.sh[:, 128 * r:128 * r + 128], T.rsh[:, 0:128], S["ha%d" % r], S.left, pid, rid, m)
+    g.wait_ge(S.left, 4 * n)
+
+
+def rank_program(g, core, T, topo):
+    S = T.sem
+    cores = list(T.cores)
+    me = T.rank_of(core)
+    if me is None:
+        for r in range(len(cores)):
+            _, far, rel = plan(cores, r, topo)
+            for k in range(len(far)):
+                if rel[k] == core:
+                    relay_program(g, core, T, topo, r, far[k])
+        return
+    near, far, rel = plan(cores, me, topo)
+    lo_f, lo_n = min(far), min(near, me)
+    on = bits(topo.mask(core, cores[near]))
+    e_lo, e_hi = on[:8], on[8:]
+    far_n = len(bits(topo.mask(rel[0], cores[far[0]])))
+
+    g.sync.dma_start(T.bt[:, 512 * lo_f:512 * lo_f + 1024], T.b[:, 512 * lo_f:512 * lo_f + 1024]).then_inc(S.ldf, 16)
+    g.sync.dma_start(T.bt[:, 512 * lo_n:512 * lo_n + 1024], T.b[:, 512 * lo_n:512 * lo_n + 1024]).then_inc(S.ldn, 16)
+    g.sync.dma_start(T.wt[:], T.w[:]).then_inc(S.ldw, 16)
+    g.sync.dma_start(T.xt[:], T.x[:]).then_inc(S.ldx, 16)
+
+    g.vector.memset(T.ones[:], 1.0).then_inc(S.one, 1)
+    g.vector.wait_ge(S.ldf, 16)
+    a = 128 * lo_f
+    g.vector.quantize_mx(T.cb[:, a:a + 256], T.sb[:, a:a + 256], T.bt[:, 4 * a:4 * a + 1024]).then_inc(S.qf, 1)
+    g.vector.wait_ge(S.ldn, 16)
+    a = 128 * lo_n
+    g.vector.quantize_mx(T.cb[:, a:a + 256], T.sb[:, a:a + 256], T.bt[:, 4 * a:4 * a + 1024]).then_inc(S.qn, 1)
+    g.vector.wait_ge(S.sel, 1)
+    for b in range(4):
+        g.vector.quantize_mx(T.cs[:, 128 * b:128 * b + 128], T.ss[:, 128 * b:128 * b + 128],
+                             T.sel[:, 3 - b:3 - b + 512]).then_inc(S.qs, 1)
+    g.vector.wait_ge(S.ldx, 16)
+    g.vector.quantize_mx(T.cx[:], T.sx[:], T.xt[:]).then_inc(S.qx, 1)
+    g.vector.wait_ge(S.ldw, 16)
+    for b in range(4):
+        g.vector.wait_ge(S["m%d" % b], 1)
+        g.vector.tensor_tensor(T.ht[:, b:512:4], T.wt[:, b:512:4], T.tm[:, 128 * b:128 * b + 128],
+                               AluOpType.subtract).then_inc(S.rr, 1)
+    g.vector.wait_ge(S.rr, 4)
+    o = 128 * me
+    g.vector.quantize_mx(T.ch[:, o:o + 128], T.sh[:, o:o + 128], T.ht[:]).then_inc(S.qh, 1)
+
+    g.wait_ge(S.one, 1)
+    g.affine_select(T.sel[:], T.ones[:], [[-1, 516]], AluOpType.is_equal, 0.0, 3, 4).then_inc(S.sel, 1)
+    left = 0
+    g.wait_ge(S.qf, 1)
+    half = [e_lo[0:4], e_lo[4:8]]
+    g.remote_dma_fused([t_send(topo, rel[k], half[k], T.sb[:, 128 * far[k]:128 * far[k] + 128], T.rsg[:, 0:128], S.rgs)
+                        for k in range(2)], local_sem=S.left)
+    g.remote_dma_fused([t_send(topo, rel[k], half[k], c8(T.cb, 128 * far[k]), c8(T.rcg, 0), S.rgc)
+                        for k in range(2)], local_sem=S.left)
+    left += 16
+    rid, pid, _ = topo.addr(cores[near])
+    g.wait_ge(S.qn, 1)
+    a = 128 * near
+    ga, ha = S["ga%d" % me], S["ha%d" % me]
+    g.remote_dma(c8(T.cg, o), c8(T.cb, a), ga, S.left, pid, rid, mask_of(e_hi))
+    g.remote_dma(T.sg[:, o:o + 128], T.sb[:, a:a + 128], ga, S.left, pid, rid, mask_of(e_hi))
+    left += 2 * len(e_hi)
+    g.wait_ge(S.qh, 1)
+    both = [e_lo, e_hi]
+    g.remote_dma_fused([t_send(topo, rel[k], both[k], c8(T.ch, o), c8(T.rch, 0), S.rhc) for k in range(2)],
+                       local_sem=S.left)
+    g.remote_dma_fused([t_send(topo, rel[k], both[k], T.sh[:, o:o + 128], T.rsh[:, 0:128], S.rhs) for k in range(2)],
+                       local_sem=S.left)
+    g.remote_dma(c8(T.ch, o), c8(T.ch, o), ha, S.left, pid, rid, mask_of(on))
+    g.remote_dma(T.sh[:, o:o + 128], T.sh[:, o:o + 128], ha, S.left, pid, rid, mask_of(on))
+    left += 4 * len(on)
+    g.wait_ge(S.left, left)
+
+    order = [me, near] + far
+    bank = {me: 4, near: 6, far[0]: 0, far[1]: 2}
+    g.tensor.wait_ge(S.qs, 4)
+    for i, r in enumerate(order):
+        if r == me:
+            g.tensor.wait_ge(S.qn, 1)
+            cq, sq = T.cb, T.sb
+        else:
+            g.tensor.wait_ge(S["ga%d" % r], 2 * (len(e_hi) if r == near else far_n))
+            cq, sq = T.cg, T.sg
+        for b in range(4):
+            mm = g.tensor.matmul_mx(T.acc[:, 512 * b:512 * b + 128], T.cs[:, 128 * b:128 * b + 128],
+                                    T.ss[:, 128 * b:128 * b + 128], cq[:, 128 * r:128 * r + 128],
+                                    sq[:, 128 * r:128 * r + 128], i == 0, i == 3)
+            if i == 3:
+                mm.then_inc(S["z%d" % b], 1)
+    g.tensor.wait_ge(S.qx, 1)
+    for j in order:
+        if j == me:
+            g.tensor.wait_ge(S.qh, 1)
+        else:
+            g.tensor.wait_ge(S["ha%d" % j], 2 * (len(on) if j == near else far_n))
+        for k in range(2):
+            c = 512 * (bank[j] + k)
+            g.tensor.matmul_mx(T.acc[:, c:c + 256], T.ch[:, 128 * j:128 * j + 128], T.sh[:, 128 * j:128 * j + 128],
+                               T.cx[:, 256 * k:256 * k + 256], T.sx[:, 256 * k:256 * k + 256],
+                               True, True).then_inc(S["p%d%d" % (j, k)], 1)
+
+    for b in range(4):
+        g.scalar.wait_ge(S["z%d" % b], 1)
+        g.scalar.activation(T.tm[:, 128 * b:128 * b + 128], T.acc[:, 512 * b:512 * b + 128],
+                            ActivationFunctionType.Copy, scale=LR).then_inc(S["m%d" % b], 1)
+    g.sync.wait_ge(S.rr, 4)
+    g.sync.dma_start(T.h[:], T.ht[:]).then_inc(S.sth, 16)
+    for j in order:
+        c, d = 512 * bank[j], 512 * j
+        g.vector.wait_ge(S["p%d0" % j], 1)
+        g.vector.tensor_copy(T.yt[:, d:d + 256], T.acc[:, c:c + 256]).then_inc(S["d%d0" % j], 1)
+        g.sync.wait_ge(S["d%d0" % j], 1)
+        g.sync.dma_start(T.y[:, d:d + 256], T.yt[:, d:d + 256]).then_inc(S.sty0, 16)
+        c, d = c + 512, d + 256
+        g.scalar.wait_ge(S["p%d1" % j], 1)
+        g.scalar.activation(T.yt[:, d:d + 256], T.acc[:, c:c + 256],
+                            ActivationFunctionType.Copy).then_inc(S["d%d1" % j], 1)
+        g.scalar.wait_ge(S["d%d1" % j], 1)
+        g.scalar.dma_start(T.y[:, d:d + 256], T.yt[:, d:d + 256]).then_inc(S.sty1, 16)
+    g.sync.wait_ge(S.sth, 16)
+    g.sync.wait_ge(S.sty0, 64)
+    g.scalar.wait_ge(S.sty1, 64)

@@ -6,27 +6,36 @@ SCRATCH = {
     "bt": ("sbuf", [128, 2048], "bfloat16"),
     "wt": ("sbuf", [128, 512], "bfloat16"),
     "xt": ("sbuf", [128, 2048], "bfloat16"),
-    "ones": ("sbuf", [128, 516], "bfloat16"),
-    "sel": ("sbuf", [128, 516], "bfloat16"),
     "ht": ("sbuf", [128, 512], "bfloat16"),
     "tm": ("sbuf", [128, 512], "float32"),
     "yt": ("sbuf", [128, 2048], "float32"),
     "cb": ("sbuf", [128, 512], F8), "sb": ("sbuf", [128, 512], "uint8"),
-    "cs": ("sbuf", [128, 512], F8), "ss": ("sbuf", [128, 512], "uint8"),
     "cx": ("sbuf", [128, 512], F8), "sx": ("sbuf", [128, 512], "uint8"),
     "cg": ("sbuf", [128, 512], F8), "sg": ("sbuf", [128, 512], "uint8"),
     "ch": ("sbuf", [128, 512], F8), "sh": ("sbuf", [128, 512], "uint8"),
     "acc": ("psum", [128, 4096], "float32"),
+    "cs": ("sbuf", [128, 512], F8), "ss": ("sbuf", [128, 512], "uint8"),
+    "ones": ("sbuf", [128, 128], "bfloat16"),
+    "sel": ("sbuf", [128, 516], "bfloat16"),
     "rcg": ("sbuf", [128, 128], F8), "rsg": ("sbuf", [128, 128], "uint8"),
     "rch": ("sbuf", [128, 128], F8), "rsh": ("sbuf", [128, 128], "uint8"),
 }
-SEMAPHORES = (["ldf", "ldn", "ldw", "ldx", "one", "sel", "qf", "qn", "qs", "qx", "rr", "qh", "sth", "left"]
-              + ["rgs", "rgc", "rhc", "rhs"]
+SEMAPHORES = (["one", "sel", "qs", "sgot", "rgs", "rgc", "rhc", "rhs", "left"]
+              + ["ld0", "ld1", "ldn", "ldw", "ldx", "q0", "q1", "qn", "qx", "rr", "qh", "sth", "sty0", "sty1"]
+              + ["lf", "ln", "lh"]
               + ["ga%d" % r for r in range(4)] + ["ha%d" % r for r in range(4)]
               + ["z%d" % b for b in range(4)] + ["m%d" % b for b in range(4)]
               + ["p%d%d" % (j, k) for j in range(4) for k in range(2)]
-              + ["d%d%d" % (j, k) for j in range(4) for k in range(2)] + ["sty0", "sty1"])
+              + ["d%d%d" % (j, k) for j in range(4) for k in range(2)])
 LR = 0.0645
+OWN_SEL = [0, 1, 2]
+RELAY_SEL = 3
+GCALLS = [["cE"], ["sE", "sL"], ["cL"]]
+HCALLS = [["cE"], ["sE"], ["cL", "cN"], ["sL", "sN"]]
+GENG = {"cE": "lo", "sE": "lo", "cL": "on", "sL": "hi", "cN": "hi", "sN": "hi"}
+HENG = {"cE": "on", "sE": "on", "cL": "lo", "sL": "lo", "cN": "hi", "sN": "hi"}
+RELAY_G = {"E": "cs", "L": "sc"}
+RELAY_H = {"E": "cs", "L": "cs"}
 
 
 def bits(m):
@@ -47,29 +56,64 @@ def plan(cores, r, topo):
     me = cores[r]
     near = [q for q in range(len(cores)) if q != r and topo.chip(cores[q]) == topo.chip(me)]
     far = [q for q in range(len(cores)) if topo.chip(cores[q]) != topo.chip(me)]
+    far.sort(key=lambda q: topo.die(cores[q]) != topo.die(me))
     hosts = [c for c in range(96) if topo.chip(c) == topo.chip(me) and topo.die(c) == topo.die(me) and c not in cores
              and all(topo.may_write(c, cores[q]) for q in far)]
     return near[0], far, hosts[:len(far)]
 
 
-def c8(t, a):
-    return t[:, a:a + 128].bitcast(dt.uint8)
+def c8(t, a, n=128):
+    return t[:, a:a + n].bitcast(dt.uint8)
 
 
-def relay_program(g, core, T, topo, r, dst):
+def engines(topo, src, dst):
+    on = bits(topo.mask(src, dst))
+    return {"on": on, "lo": on[:len(on) // 2], "hi": on[len(on) // 2:]}
+
+
+def fill_sel(g, T):
+    g.vector.memset(T.ones[:], 1.0).then_inc(T.sem.one, 1)
+    g.vector.memset(T.sel[:], 0.0).then_inc(T.sem.one, 1)
+    g.wait_ge(T.sem.one, 2)
+    g.affine_select(T.sel[:, 3:515:4], T.ones[:], [[-1, 128]], AluOpType.is_equal, 0.0, 0, 1).then_inc(T.sem.sel, 1)
+
+
+def quant_sel(g, T, which):
+    g.vector.wait_ge(T.sem.sel, 1)
+    for b in which:
+        g.vector.quantize_mx(T.cs[:, 128 * b:128 * b + 128], T.ss[:, 128 * b:128 * b + 128],
+                             T.sel[:, 3 - b:3 - b + 512]).then_inc(T.sem.qs, 1)
+
+
+def relay_program(g, core, T, topo, r, k, dst):
     S = T.sem
-    es = bits(topo.mask(core, T.cores[dst]))
+    on = engines(topo, T.cores[r], core)
+    m = topo.mask(core, T.cores[dst])
+    n = len(bits(m))
+    fill_sel(g, T)
+    quant_sel(g, T, [RELAY_SEL])
+    rid, pid, _ = topo.addr(T.cores[r])
+    a = 128 * RELAY_SEL + 64 * k
+    g.wait_ge(S.qs, 1)
+    g.remote_dma(c8(T.cs, a, 64), c8(T.cs, a, 64), S.sgot, S.left, pid, rid, m)
+    g.remote_dma(T.ss[:, a:a + 64], T.ss[:, a:a + 64], S.sgot, S.left, pid, rid, m)
     rid, pid, _ = topo.addr(T.cores[dst])
-    m, n = mask_of(es), len(es)
-    g.wait_ge(S.rgs, 4)
-    g.remote_dma(T.sg[:, 128 * r:128 * r + 128], T.rsg[:, 0:128], S["ga%d" % r], S.left, pid, rid, m)
-    g.wait_ge(S.rgc, 4)
-    g.remote_dma(c8(T.cg, 128 * r), c8(T.rcg, 0), S["ga%d" % r], S.left, pid, rid, m)
-    g.wait_ge(S.rhc, 8)
-    g.remote_dma(c8(T.ch, 128 * r), c8(T.rch, 0), S["ha%d" % r], S.left, pid, rid, m)
-    g.wait_ge(S.rhs, 8)
-    g.remote_dma(T.sh[:, 128 * r:128 * r + 128], T.rsh[:, 0:128], S["ha%d" % r], S.left, pid, rid, m)
-    g.wait_ge(S.left, 4 * n)
+    who, o = "EL"[k], 128 * r
+    for ch in RELAY_G[who]:
+        if ch == "s":
+            g.wait_ge(S.rgs, len(on[GENG["s" + who]]))
+            g.remote_dma(T.sg[:, o:o + 128], T.rsg[:, 0:128], S["ga%d" % r], S.left, pid, rid, m)
+        else:
+            g.wait_ge(S.rgc, len(on[GENG["c" + who]]))
+            g.remote_dma(c8(T.cg, o), c8(T.rcg, 0), S["ga%d" % r], S.left, pid, rid, m)
+    for ch in RELAY_H[who]:
+        if ch == "s":
+            g.wait_ge(S.rhs, len(on[HENG["s" + who]]))
+            g.remote_dma(T.sh[:, o:o + 128], T.rsh[:, 0:128], S["ha%d" % r], S.left, pid, rid, m)
+        else:
+            g.wait_ge(S.rhc, len(on[HENG["c" + who]]))
+            g.remote_dma(c8(T.ch, o), c8(T.rch, 0), S["ha%d" % r], S.left, pid, rid, m)
+    g.wait_ge(S.left, 6 * n)
 
 
 def rank_program(g, core, T, topo):
@@ -81,115 +125,132 @@ def rank_program(g, core, T, topo):
             _, far, rel = plan(cores, r, topo)
             for k in range(len(far)):
                 if rel[k] == core:
-                    relay_program(g, core, T, topo, r, far[k])
+                    relay_program(g, core, T, topo, r, k, far[k])
         return
     near, far, rel = plan(cores, me, topo)
-    lo_f, lo_n = min(far), min(near, me)
-    on = bits(topo.mask(core, cores[near]))
-    e_lo, e_hi = on[:8], on[8:]
+    lo_n = min(near, me)
+    on = engines(topo, core, cores[near])
     far_n = len(bits(topo.mask(rel[0], cores[far[0]])))
-
-    g.sync.dma_start(T.bt[:, 512 * lo_f:512 * lo_f + 1024], T.b[:, 512 * lo_f:512 * lo_f + 1024]).then_inc(S.ldf, 16)
-    g.sync.dma_start(T.bt[:, 512 * lo_n:512 * lo_n + 1024], T.b[:, 512 * lo_n:512 * lo_n + 1024]).then_inc(S.ldn, 16)
-    g.sync.dma_start(T.wt[:], T.w[:]).then_inc(S.ldw, 16)
-    g.sync.dma_start(T.xt[:], T.x[:]).then_inc(S.ldx, 16)
-
-    g.vector.memset(T.ones[:], 1.0).then_inc(S.one, 1)
-    g.vector.wait_ge(S.ldf, 16)
-    a = 128 * lo_f
-    g.vector.quantize_mx(T.cb[:, a:a + 256], T.sb[:, a:a + 256], T.bt[:, 4 * a:4 * a + 1024]).then_inc(S.qf, 1)
-    g.vector.wait_ge(S.ldn, 16)
-    a = 128 * lo_n
-    g.vector.quantize_mx(T.cb[:, a:a + 256], T.sb[:, a:a + 256], T.bt[:, 4 * a:4 * a + 1024]).then_inc(S.qn, 1)
-    g.vector.wait_ge(S.sel, 1)
-    for b in range(4):
-        g.vector.quantize_mx(T.cs[:, 128 * b:128 * b + 128], T.ss[:, 128 * b:128 * b + 128],
-                             T.sel[:, 3 - b:3 - b + 512]).then_inc(S.qs, 1)
-    g.vector.wait_ge(S.ldx, 16)
-    g.vector.quantize_mx(T.cx[:], T.sx[:], T.xt[:]).then_inc(S.qx, 1)
-    g.vector.wait_ge(S.ldw, 16)
-    for b in range(4):
-        g.vector.wait_ge(S["m%d" % b], 1)
-        g.vector.tensor_tensor(T.ht[:, b:512:4], T.wt[:, b:512:4], T.tm[:, 128 * b:128 * b + 128],
-                               AluOpType.subtract).then_inc(S.rr, 1)
-    g.vector.wait_ge(S.rr, 4)
+    v, t, s, y = g.vector, g.tensor, g.scalar, g.sync
     o = 128 * me
-    g.vector.quantize_mx(T.ch[:, o:o + 128], T.sh[:, o:o + 128], T.ht[:]).then_inc(S.qh, 1)
 
-    g.wait_ge(S.one, 1)
-    g.affine_select(T.sel[:], T.ones[:], [[-1, 516]], AluOpType.is_equal, 0.0, 3, 4).then_inc(S.sel, 1)
-    left = 0
-    g.wait_ge(S.qf, 1)
-    half = [e_lo[0:4], e_lo[4:8]]
-    g.remote_dma_fused([t_send(topo, rel[k], half[k], T.sb[:, 128 * far[k]:128 * far[k] + 128], T.rsg[:, 0:128], S.rgs)
-                        for k in range(2)], local_sem=S.left)
-    g.remote_dma_fused([t_send(topo, rel[k], half[k], c8(T.cb, 128 * far[k]), c8(T.rcg, 0), S.rgc)
-                        for k in range(2)], local_sem=S.left)
-    left += 16
-    rid, pid, _ = topo.addr(cores[near])
-    g.wait_ge(S.qn, 1)
-    a = 128 * near
     ga, ha = S["ga%d" % me], S["ha%d" % me]
-    g.remote_dma(c8(T.cg, o), c8(T.cb, a), ga, S.left, pid, rid, mask_of(e_hi))
-    g.remote_dma(T.sg[:, o:o + 128], T.sb[:, a:a + 128], ga, S.left, pid, rid, mask_of(e_hi))
-    left += 2 * len(e_hi)
+    dst = {"E": rel[0], "L": rel[1], "N": cores[near]}
+    tile = {"E": 128 * far[0], "L": 128 * far[1], "N": 128 * near}
+
+    def send_g(c):
+        kind, d = c
+        a, es = tile[d], on[GENG[c]]
+        if kind == "c":
+            to, sem = (c8(T.cg, o), ga) if d == "N" else (c8(T.rcg, 0), S.rgc)
+            return t_send(topo, dst[d], es, c8(T.cb, a), to, sem)
+        to, sem = (T.sg[:, o:o + 128], ga) if d == "N" else (T.rsg[:, 0:128], S.rgs)
+        return t_send(topo, dst[d], es, T.sb[:, a:a + 128], to, sem)
+
+    def send_h(c):
+        kind, d = c
+        es = on[HENG[c]]
+        if kind == "c":
+            to, sem = (c8(T.ch, o), ha) if d == "N" else (c8(T.rch, 0), S.rhc)
+            return t_send(topo, dst[d], es, c8(T.ch, o), to, sem)
+        to, sem = (T.sh[:, o:o + 128], ha) if d == "N" else (T.rsh[:, 0:128], S.rhs)
+        return t_send(topo, dst[d], es, T.sh[:, o:o + 128], to, sem)
+
+    def load_b(c, n, sem):
+        y.dma_start(T.bt[:, 512 * c:512 * (c + n)], T.b[:, 512 * c:512 * (c + n)]).then_inc(sem, 16)
+
+    load_b(far[0], 1, S.ld0)
+    load_b(far[1], 1, S.ld1)
+    y.wait_ge(S.ld0, 16)
+    load_b(lo_n, 2, S.ldn)
+    y.wait_ge(S.lf, sum(len(on[GENG[c]]) for call in GCALLS for c in call))
+    y.dma_start(T.wt[:], T.w[:]).then_inc(S.ldw, 16)
+    y.dma_start(T.xt[:], T.x[:]).then_inc(S.ldx, 16)
+
+    def quant_b(c, n, sem):
+        v.quantize_mx(T.cb[:, 128 * c:128 * (c + n)], T.sb[:, 128 * c:128 * (c + n)],
+                      T.bt[:, 512 * c:512 * (c + n)]).then_inc(sem, 1)
+
+    fill_sel(g, T)
+    v.wait_ge(S.ld0, 16)
+    quant_b(far[0], 1, S.q0)
+    v.wait_ge(S.ld1, 16)
+    quant_b(far[1], 1, S.q1)
+    v.wait_ge(S.ldn, 16)
+    quant_b(lo_n, 2, S.qn)
+    quant_sel(g, T, OWN_SEL)
+    v.wait_ge(S.ldw, 16)
+    for b in range(4):
+        v.wait_ge(S["m%d" % b], 1)
+        v.tensor_tensor(T.ht[:, b:512:4], T.wt[:, b:512:4], T.tm[:, 128 * b:128 * b + 128],
+                        AluOpType.subtract).then_inc(S.rr, 1)
+    v.wait_ge(S.rr, 4)
+    v.quantize_mx(T.ch[:, o:o + 128], T.sh[:, o:o + 128], T.ht[:]).then_inc(S.qh, 1)
+    v.wait_ge(S.ldx, 16)
+    v.quantize_mx(T.cx[:], T.sx[:], T.xt[:]).then_inc(S.qx, 1)
+
+    ready = {"E": S.q0, "L": S.q1}
+    for call in GCALLS:
+        for c in call:
+            g.wait_ge(ready[c[1]], 1)
+        g.remote_dma_fused([send_g(c) for c in call], local_sem=S.lf)
+    g.wait_ge(S.qn, 1)
+    g.remote_dma_fused([send_g("cN")], local_sem=S.ln)
+    g.remote_dma_fused([send_g("sN")], local_sem=S.ln)
     g.wait_ge(S.qh, 1)
-    both = [e_lo, e_hi]
-    g.remote_dma_fused([t_send(topo, rel[k], both[k], c8(T.ch, o), c8(T.rch, 0), S.rhc) for k in range(2)],
-                       local_sem=S.left)
-    g.remote_dma_fused([t_send(topo, rel[k], both[k], T.sh[:, o:o + 128], T.rsh[:, 0:128], S.rhs) for k in range(2)],
-                       local_sem=S.left)
-    g.remote_dma(c8(T.ch, o), c8(T.ch, o), ha, S.left, pid, rid, mask_of(on))
-    g.remote_dma(T.sh[:, o:o + 128], T.sh[:, o:o + 128], ha, S.left, pid, rid, mask_of(on))
-    left += 4 * len(on)
-    g.wait_ge(S.left, left)
+    for call in HCALLS:
+        g.remote_dma_fused([send_h(c) for c in call], local_sem=S.lh)
+    g.wait_ge(S.ln, len(on[GENG["cN"]]) + len(on[GENG["sN"]]))
+    g.wait_ge(S.lh, sum(len(on[HENG[c]]) for call in HCALLS for c in call))
 
     order = [me, near] + far
-    bank = {me: 4, near: 6, far[0]: 0, far[1]: 2}
-    g.tensor.wait_ge(S.qs, 4)
+    got_g = {near: len(on[GENG["cN"]]) + len(on[GENG["sN"]]), far[0]: 2 * far_n, far[1]: 2 * far_n}
+    got_h = {near: len(on[HENG["cN"]]) + len(on[HENG["sN"]]), far[0]: 2 * far_n, far[1]: 2 * far_n}
+    t.wait_ge(S.qs, len(OWN_SEL))
+    t.wait_ge(S.sgot, 4 * far_n)
     for i, r in enumerate(order):
         if r == me:
-            g.tensor.wait_ge(S.qn, 1)
+            t.wait_ge(S.qn, 1)
             cq, sq = T.cb, T.sb
         else:
-            g.tensor.wait_ge(S["ga%d" % r], 2 * (len(e_hi) if r == near else far_n))
+            t.wait_ge(S["ga%d" % r], got_g[r])
             cq, sq = T.cg, T.sg
         for b in range(4):
-            mm = g.tensor.matmul_mx(T.acc[:, 512 * b:512 * b + 128], T.cs[:, 128 * b:128 * b + 128],
-                                    T.ss[:, 128 * b:128 * b + 128], cq[:, 128 * r:128 * r + 128],
-                                    sq[:, 128 * r:128 * r + 128], i == 0, i == 3)
+            mm = t.matmul_mx(T.acc[:, 512 * b:512 * b + 128], T.cs[:, 128 * b:128 * b + 128],
+                             T.ss[:, 128 * b:128 * b + 128], cq[:, 128 * r:128 * r + 128],
+                             sq[:, 128 * r:128 * r + 128], i == 0, i == 3)
             if i == 3:
                 mm.then_inc(S["z%d" % b], 1)
-    g.tensor.wait_ge(S.qx, 1)
-    for j in order:
-        if j == me:
-            g.tensor.wait_ge(S.qh, 1)
-        else:
-            g.tensor.wait_ge(S["ha%d" % j], 2 * (len(on) if j == near else far_n))
-        for k in range(2):
-            c = 512 * (bank[j] + k)
-            g.tensor.matmul_mx(T.acc[:, c:c + 256], T.ch[:, 128 * j:128 * j + 128], T.sh[:, 128 * j:128 * j + 128],
-                               T.cx[:, 256 * k:256 * k + 256], T.sx[:, 256 * k:256 * k + 256],
-                               True, True).then_inc(S["p%d%d" % (j, k)], 1)
 
     for b in range(4):
-        g.scalar.wait_ge(S["z%d" % b], 1)
-        g.scalar.activation(T.tm[:, 128 * b:128 * b + 128], T.acc[:, 512 * b:512 * b + 128],
-                            ActivationFunctionType.Copy, scale=LR).then_inc(S["m%d" % b], 1)
-    g.sync.wait_ge(S.rr, 4)
-    g.sync.dma_start(T.h[:], T.ht[:]).then_inc(S.sth, 16)
+        s.wait_ge(S["z%d" % b], 1)
+        s.activation(T.tm[:, 128 * b:128 * b + 128], T.acc[:, 512 * b:512 * b + 128],
+                     ActivationFunctionType.Copy, scale=LR).then_inc(S["m%d" % b], 1)
+
+    bank = {me: 4, near: 6, far[0]: 0, far[1]: 2}
+    t.wait_ge(S.qx, 1)
     for j in order:
+        if j == me:
+            t.wait_ge(S.qh, 1)
+        else:
+            t.wait_ge(S["ha%d" % j], got_h[j])
         c, d = 512 * bank[j], 512 * j
-        g.vector.wait_ge(S["p%d0" % j], 1)
-        g.vector.tensor_copy(T.yt[:, d:d + 256], T.acc[:, c:c + 256]).then_inc(S["d%d0" % j], 1)
-        g.sync.wait_ge(S["d%d0" % j], 1)
-        g.sync.dma_start(T.y[:, d:d + 256], T.yt[:, d:d + 256]).then_inc(S.sty0, 16)
+        for k in range(2):
+            t.matmul_mx(T.acc[:, c + 512 * k:c + 512 * k + 256], T.ch[:, 128 * j:128 * j + 128],
+                        T.sh[:, 128 * j:128 * j + 128], T.cx[:, 256 * k:256 * k + 256],
+                        T.sx[:, 256 * k:256 * k + 256], True, True).then_inc(S["p%d%d" % (j, k)], 1)
+        v.wait_ge(S["p%d0" % j], 1)
+        v.tensor_copy(T.yt[:, d:d + 256], T.acc[:, c:c + 256]).then_inc(S["d%d0" % j], 1)
+        y.wait_ge(S["d%d0" % j], 1)
+        y.dma_start(T.y[:, d:d + 256], T.yt[:, d:d + 256]).then_inc(S.sty0, 16)
+        if j == me:
+            y.wait_ge(S.rr, 4)
+            y.dma_start(T.h[:], T.ht[:]).then_inc(S.sth, 16)
         c, d = c + 512, d + 256
-        g.scalar.wait_ge(S["p%d1" % j], 1)
-        g.scalar.activation(T.yt[:, d:d + 256], T.acc[:, c:c + 256],
-                            ActivationFunctionType.Copy).then_inc(S["d%d1" % j], 1)
-        g.scalar.wait_ge(S["d%d1" % j], 1)
-        g.scalar.dma_start(T.y[:, d:d + 256], T.yt[:, d:d + 256]).then_inc(S.sty1, 16)
-    g.sync.wait_ge(S.sth, 16)
-    g.sync.wait_ge(S.sty0, 64)
-    g.scalar.wait_ge(S.sty1, 64)
+        s.wait_ge(S["p%d1" % j], 1)
+        s.activation(T.yt[:, d:d + 256], T.acc[:, c:c + 256], ActivationFunctionType.Copy).then_inc(S["d%d1" % j], 1)
+        s.wait_ge(S["d%d1" % j], 1)
+        s.dma_start(T.y[:, d:d + 256], T.yt[:, d:d + 256]).then_inc(S.sty1, 16)
+    y.wait_ge(S.sth, 16)
+    y.wait_ge(S.sty0, 64)
+    s.wait_ge(S.sty1, 64)

from concourse.bass import DstId, RemoteDMATransfer
from concourse.mybir import dt, AluOpType, ActivationFunctionType

F8 = "float8_e4m3fn_x4"
SCRATCH = {
    "bt": ("sbuf", [128, 2048], "bfloat16"),
    "wt": ("sbuf", [128, 512], "bfloat16"),
    "xt": ("sbuf", [128, 2048], "bfloat16"),
    "ht": ("sbuf", [128, 512], "bfloat16"),
    "tm": ("sbuf", [128, 512], "float32"),
    "yt": ("sbuf", [128, 2048], "float32"),
    "cb": ("sbuf", [128, 512], F8), "sb": ("sbuf", [128, 512], "uint8"),
    "cx": ("sbuf", [128, 512], F8), "sx": ("sbuf", [128, 512], "uint8"),
    "cg": ("sbuf", [128, 512], F8), "sg": ("sbuf", [128, 512], "uint8"),
    "ch": ("sbuf", [128, 512], F8), "sh": ("sbuf", [128, 512], "uint8"),
    "acc": ("psum", [128, 4096], "float32"),
    "cs": ("sbuf", [128, 512], F8), "ss": ("sbuf", [128, 512], "uint8"),
    "ones": ("sbuf", [128, 128], "bfloat16"),
    "sel": ("sbuf", [128, 516], "bfloat16"),
    "rcg": ("sbuf", [128, 128], F8), "rsg": ("sbuf", [128, 128], "uint8"),
    "rch": ("sbuf", [128, 128], F8), "rsh": ("sbuf", [128, 128], "uint8"),
}
SEMAPHORES = (["one", "sel", "qs", "sgot", "rgs", "rgc", "rhc", "rhs", "left"]
              + ["ld0", "ld1", "ldn", "ldw", "ldx", "q0", "q1", "qn", "qx", "rr", "qh", "sth", "sty0", "sty1"]
              + ["lf", "ln", "lh"]
              + ["ga%d" % r for r in range(4)] + ["ha%d" % r for r in range(4)]
              + ["z%d" % b for b in range(4)] + ["m%d" % b for b in range(4)]
              + ["p%d%d" % (j, k) for j in range(4) for k in range(2)]
              + ["d%d%d" % (j, k) for j in range(4) for k in range(2)])
LR = 0.0645
OWN_SEL = [0, 1, 2]
RELAY_SEL = 3
GCALLS = [["cE"], ["sE", "sL"], ["cL"]]
HCALLS = [["cE"], ["sE"], ["cL", "cN"], ["sL", "sN"]]
GENG = {"cE": "lo", "sE": "lo", "cL": "on", "sL": "hi", "cN": "hi", "sN": "hi"}
HENG = {"cE": "on", "sE": "on", "cL": "lo", "sL": "lo", "cN": "hi", "sN": "hi"}
RELAY_G = {"E": "cs", "L": "sc"}
RELAY_H = {"E": "cs", "L": "cs"}


def bits(m):
    return [i for i in range(m.bit_length()) if (m >> i) & 1]


def mask_of(es):
    return sum(1 << e for e in es)


def t_send(topo, dst, es, src_ap, dst_ap, sem):
    rid, pid, _ = topo.addr(dst)
    return RemoteDMATransfer(dst_ids=[DstId(rid=rid, pnc=pid)], dma_engine_mask=mask_of(es), remote_sem=sem,
                             src=src_ap, dst=dst_ap)


def plan(cores, r, topo):
    me = cores[r]
    near = [q for q in range(len(cores)) if q != r and topo.chip(cores[q]) == topo.chip(me)]
    far = [q for q in range(len(cores)) if topo.chip(cores[q]) != topo.chip(me)]
    far.sort(key=lambda q: topo.die(cores[q]) != topo.die(me))
    hosts = [c for c in range(96) if topo.chip(c) == topo.chip(me) and topo.die(c) == topo.die(me) and c not in cores
             and all(topo.may_write(c, cores[q]) for q in far)]
    return near[0], far, hosts[:len(far)]


def c8(t, a, n=128):
    return t[:, a:a + n].bitcast(dt.uint8)


def engines(topo, src, dst):
    on = bits(topo.mask(src, dst))
    return {"on": on, "lo": on[:len(on) // 2], "hi": on[len(on) // 2:]}


def fill_sel(g, T):
    g.vector.memset(T.ones[:], 1.0).then_inc(T.sem.one, 1)
    g.vector.memset(T.sel[:], 0.0).then_inc(T.sem.one, 1)
    g.wait_ge(T.sem.one, 2)
    g.affine_select(T.sel[:, 3:515:4], T.ones[:], [[-1, 128]], AluOpType.is_equal, 0.0, 0, 1).then_inc(T.sem.sel, 1)


def quant_sel(g, T, which):
    g.vector.wait_ge(T.sem.sel, 1)
    for b in which:
        g.vector.quantize_mx(T.cs[:, 128 * b:128 * b + 128], T.ss[:, 128 * b:128 * b + 128],
                             T.sel[:, 3 - b:3 - b + 512]).then_inc(T.sem.qs, 1)


def relay_program(g, core, T, topo, r, k, dst):
    S = T.sem
    on = engines(topo, T.cores[r], core)
    m = topo.mask(core, T.cores[dst])
    n = len(bits(m))
    fill_sel(g, T)
    quant_sel(g, T, [RELAY_SEL])
    rid, pid, _ = topo.addr(T.cores[r])
    a = 128 * RELAY_SEL + 64 * k
    g.wait_ge(S.qs, 1)
    g.remote_dma(c8(T.cs, a, 64), c8(T.cs, a, 64), S.sgot, S.left, pid, rid, m)
    g.remote_dma(T.ss[:, a:a + 64], T.ss[:, a:a + 64], S.sgot, S.left, pid, rid, m)
    rid, pid, _ = topo.addr(T.cores[dst])
    who, o = "EL"[k], 128 * r
    for ch in RELAY_G[who]:
        if ch == "s":
            g.wait_ge(S.rgs, len(on[GENG["s" + who]]))
            g.remote_dma(T.sg[:, o:o + 128], T.rsg[:, 0:128], S["ga%d" % r], S.left, pid, rid, m)
        else:
            g.wait_ge(S.rgc, len(on[GENG["c" + who]]))
            g.remote_dma(c8(T.cg, o), c8(T.rcg, 0), S["ga%d" % r], S.left, pid, rid, m)
    for ch in RELAY_H[who]:
        if ch == "s":
            g.wait_ge(S.rhs, len(on[HENG["s" + who]]))
            g.remote_dma(T.sh[:, o:o + 128], T.rsh[:, 0:128], S["ha%d" % r], S.left, pid, rid, m)
        else:
            g.wait_ge(S.rhc, len(on[HENG["c" + who]]))
            g.remote_dma(c8(T.ch, o), c8(T.rch, 0), S["ha%d" % r], S.left, pid, rid, m)
    g.wait_ge(S.left, 6 * n)


def rank_program(g, core, T, topo):
    S = T.sem
    cores = list(T.cores)
    me = T.rank_of(core)
    if me is None:
        for r in range(len(cores)):
            _, far, rel = plan(cores, r, topo)
            for k in range(len(far)):
                if rel[k] == core:
                    relay_program(g, core, T, topo, r, k, far[k])
        return
    near, far, rel = plan(cores, me, topo)
    lo_n = min(near, me)
    on = engines(topo, core, cores[near])
    far_n = len(bits(topo.mask(rel[0], cores[far[0]])))
    v, t, s, y = g.vector, g.tensor, g.scalar, g.sync
    o = 128 * me

    ga, ha = S["ga%d" % me], S["ha%d" % me]
    dst = {"E": rel[0], "L": rel[1], "N": cores[near]}
    tile = {"E": 128 * far[0], "L": 128 * far[1], "N": 128 * near}

    def send_g(c):
        kind, d = c
        a, es = tile[d], on[GENG[c]]
        if kind == "c":
            to, sem = (c8(T.cg, o), ga) if d == "N" else (c8(T.rcg, 0), S.rgc)
            return t_send(topo, dst[d], es, c8(T.cb, a), to, sem)
        to, sem = (T.sg[:, o:o + 128], ga) if d == "N" else (T.rsg[:, 0:128], S.rgs)
        return t_send(topo, dst[d], es, T.sb[:, a:a + 128], to, sem)

    def send_h(c):
        kind, d = c
        es = on[HENG[c]]
        if kind == "c":
            to, sem = (c8(T.ch, o), ha) if d == "N" else (c8(T.rch, 0), S.rhc)
            return t_send(topo, dst[d], es, c8(T.ch, o), to, sem)
        to, sem = (T.sh[:, o:o + 128], ha) if d == "N" else (T.rsh[:, 0:128], S.rhs)
        return t_send(topo, dst[d], es, T.sh[:, o:o + 128], to, sem)

    def load_b(c, n, sem):
        y.dma_start(T.bt[:, 512 * c:512 * (c + n)], T.b[:, 512 * c:512 * (c + n)]).then_inc(sem, 16)

    load_b(far[0], 1, S.ld0)
    load_b(far[1], 1, S.ld1)
    y.wait_ge(S.ld0, 16)
    load_b(lo_n, 2, S.ldn)
    y.wait_ge(S.lf, sum(len(on[GENG[c]]) for call in GCALLS for c in call))
    y.dma_start(T.wt[:], T.w[:]).then_inc(S.ldw, 16)
    y.dma_start(T.xt[:], T.x[:]).then_inc(S.ldx, 16)

    def quant_b(c, n, sem):
        v.quantize_mx(T.cb[:, 128 * c:128 * (c + n)], T.sb[:, 128 * c:128 * (c + n)],
                      T.bt[:, 512 * c:512 * (c + n)]).then_inc(sem, 1)

    fill_sel(g, T)
    v.wait_ge(S.ld0, 16)
    quant_b(far[0], 1, S.q0)
    v.wait_ge(S.ld1, 16)
    quant_b(far[1], 1, S.q1)
    v.wait_ge(S.ldn, 16)
    quant_b(lo_n, 2, S.qn)
    quant_sel(g, T, OWN_SEL)
    v.wait_ge(S.ldw, 16)
    for b in range(4):
        v.wait_ge(S["m%d" % b], 1)
        v.tensor_tensor(T.ht[:, b:512:4], T.wt[:, b:512:4], T.tm[:, 128 * b:128 * b + 128],
                        AluOpType.subtract).then_inc(S.rr, 1)
    v.wait_ge(S.rr, 4)
    v.quantize_mx(T.ch[:, o:o + 128], T.sh[:, o:o + 128], T.ht[:]).then_inc(S.qh, 1)
    v.wait_ge(S.ldx, 16)
    v.quantize_mx(T.cx[:], T.sx[:], T.xt[:]).then_inc(S.qx, 1)

    ready = {"E": S.q0, "L": S.q1}
    for call in GCALLS:
        for c in call:
            g.wait_ge(ready[c[1]], 1)
        g.remote_dma_fused([send_g(c) for c in call], local_sem=S.lf)
    g.wait_ge(S.qn, 1)
    g.remote_dma_fused([send_g("cN")], local_sem=S.ln)
    g.remote_dma_fused([send_g("sN")], local_sem=S.ln)
    g.wait_ge(S.qh, 1)
    for call in HCALLS:
        g.remote_dma_fused([send_h(c) for c in call], local_sem=S.lh)
    g.wait_ge(S.ln, len(on[GENG["cN"]]) + len(on[GENG["sN"]]))
    g.wait_ge(S.lh, sum(len(on[HENG[c]]) for call in HCALLS for c in call))

    order = [me, near] + far
    got_g = {near: len(on[GENG["cN"]]) + len(on[GENG["sN"]]), far[0]: 2 * far_n, far[1]: 2 * far_n}
    got_h = {near: len(on[HENG["cN"]]) + len(on[HENG["sN"]]), far[0]: 2 * far_n, far[1]: 2 * far_n}
    t.wait_ge(S.qs, len(OWN_SEL))
    t.wait_ge(S.sgot, 4 * far_n)
    for i, r in enumerate(order):
        if r == me:
            t.wait_ge(S.qn, 1)
            cq, sq = T.cb, T.sb
        else:
            t.wait_ge(S["ga%d" % r], got_g[r])
            cq, sq = T.cg, T.sg
        for b in range(4):
            mm = t.matmul_mx(T.acc[:, 512 * b:512 * b + 128], T.cs[:, 128 * b:128 * b + 128],
                             T.ss[:, 128 * b:128 * b + 128], cq[:, 128 * r:128 * r + 128],
                             sq[:, 128 * r:128 * r + 128], i == 0, i == 3)
            if i == 3:
                mm.then_inc(S["z%d" % b], 1)

    for b in range(4):
        s.wait_ge(S["z%d" % b], 1)
        s.activation(T.tm[:, 128 * b:128 * b + 128], T.acc[:, 512 * b:512 * b + 128],
                     ActivationFunctionType.Copy, scale=LR).then_inc(S["m%d" % b], 1)

    bank = {me: 4, near: 6, far[0]: 0, far[1]: 2}
    t.wait_ge(S.qx, 1)
    for j in order:
        if j == me:
            t.wait_ge(S.qh, 1)
        else:
            t.wait_ge(S["ha%d" % j], got_h[j])
        c, d = 512 * bank[j], 512 * j
        for k in range(2):
            t.matmul_mx(T.acc[:, c + 512 * k:c + 512 * k + 256], T.ch[:, 128 * j:128 * j + 128],
                        T.sh[:, 128 * j:128 * j + 128], T.cx[:, 256 * k:256 * k + 256],
                        T.sx[:, 256 * k:256 * k + 256], True, True).then_inc(S["p%d%d" % (j, k)], 1)
        v.wait_ge(S["p%d0" % j], 1)
        v.tensor_copy(T.yt[:, d:d + 256], T.acc[:, c:c + 256]).then_inc(S["d%d0" % j], 1)
        y.wait_ge(S["d%d0" % j], 1)
        y.dma_start(T.y[:, d:d + 256], T.yt[:, d:d + 256]).then_inc(S.sty0, 16)
        if j == me:
            y.wait_ge(S.rr, 4)
            y.dma_start(T.h[:], T.ht[:]).then_inc(S.sth, 16)
        c, d = c + 512, d + 256
        s.wait_ge(S["p%d1" % j], 1)
        s.activation(T.yt[:, d:d + 256], T.acc[:, c:c + 256], ActivationFunctionType.Copy).then_inc(S["d%d1" % j], 1)
        s.wait_ge(S["d%d1" % j], 1)
        s.dma_start(T.y[:, d:d + 256], T.yt[:, d:d + 256]).then_inc(S.sty1, 16)
    y.wait_ge(S.sth, 16)
    y.wait_ge(S.sty0, 64)
    s.wait_ge(S.sty1, 64)
